import numpy as np
import ml_dtypes


def mxq(x, axis, fmt="e4m3"):
    dtype, down = {"e4m3": (ml_dtypes.float8_e4m3fn, 7), "e5m2": (ml_dtypes.float8_e5m2, 14)}[fmt]
    v = np.moveaxis(np.asarray(x, np.float32).astype(ml_dtypes.bfloat16).astype(np.float64), axis, -1)
    blocks = v.reshape(v.shape[:-1] + (-1, 32))
    amax = np.abs(blocks).max(-1, keepdims=True)
    byte = np.maximum(np.where(amax > 0, np.frexp(amax)[1] - 1 + 127, 0) - down, 1)
    scale = np.exp2(byte - 127.0)
    codes = (blocks / scale).astype(np.float32).astype(dtype).astype(np.float64)
    return np.moveaxis((codes * scale).reshape(v.shape), -1, axis)


WIDE = False


def mx_kscale(k):
    if not WIDE:
        return np.ones(k)
    levels = np.array([10, -10, 5, -5, 0])
    if k % 512:
        return np.exp2(np.random.permutation(np.resize(levels, k // 32))).repeat(32)
    a = np.empty((k // 512, 16))
    for p in range(k // 512):
        a[p, :8] = np.random.permutation(np.resize(levels, 8))
        for g in range(8):
            far = levels[np.abs(levels - a[p, g]) >= 10]
            a[p, g + 8] = far[np.random.randint(len(far))]
    return np.exp2(a.ravel()).repeat(32)


def f64(x):
    return np.asarray(x).astype(np.float64)


def striped(idx):
    return np.tile(idx.reshape(-1, 16).T, (8, 1)).astype(np.uint16)


def unstriped(offs):
    return offs[:16].T.reshape(-1).astype(np.int64)


def relu(v):
    return np.maximum(v, 0.0)


K, T, S, V, H, N = 512, 2048, 768, 1536, 1024, 512
P = 2 ** 7


def setup_inputs():
    n = np.random.standard_normal
    s = mx_kscale(K)[:, None]
    u = mx_kscale(H)
    return {
        "xT": (n((K, T)) * s).astype(np.float32),
        "w1": (n((K, H)) / np.sqrt(K) / s * u).astype(np.float32),
        "w2": (n((H, N)) / np.sqrt(H) / u[:, None]).astype(np.float32),
        "gate": np.tile(np.random.uniform(0.5, 1.5, S), (P, 1)).astype(np.float32),
        "offs": striped(np.random.permutation(T)[:S]),
        "pos1": striped(np.random.permutation(V)[:S]),
    }


def reference(xT, w1, w2, gate, offs, pos1):
    h = relu(mxq(f64(w1), 0, "e4m3").T @ mxq(f64(xT)[:, unstriped(offs)], 0, "e4m3"))
    z = np.zeros((H, V))
    z[:, unstriped(pos1)] = f64(gate)[:1] * h
    return mxq(f64(w2), 0, "e4m3").T @ mxq(z, 0, "e4m3")

from contextlib import ExitStack

import concourse.mybir as mybir

K, T, S, V, H, N = 512, 2048, 768, 1536, 1024, 512
FLOPS = 2 * K * H * S + 2 * H * N * V

F32 = mybir.dt.float32
BF16 = mybir.dt.bfloat16
U32 = mybir.dt.uint32
U16 = mybir.dt.uint16
U8 = mybir.dt.uint8
FP8X4 = mybir.dt.float8_e4m3fn_x4
COPY = mybir.ActivationFunctionType.Copy
RELU = mybir.ActivationFunctionType.Relu
MULT = mybir.AluOpType.mult

P = 128
PACK = 4
HALF = P * PACK
PIECES = ((0, 256), (256, 768))
CHUNKS = ((0, 256), (256, 512), (512, 1024), (1024, 1536))


def tile_picked_voxel_relu_e_kernel(tc, xT, w1, w2, gate, offs, pos1, out):
    nc = tc.nc
    x_view = xT.rearrange("(p j) t -> p j t", j=PACK)
    w1_view = w1.rearrange("(p j) c -> p j c", j=PACK)
    out_view = out.rearrange("(m p) v -> p m v", p=P)

    def quantize(codes, scales, grouped):
        nc.vector.quantize_mx(out=codes.bitcast(FP8X4), scales=scales, in_=grouped.rearrange("p w j -> p (w j)"))

    with ExitStack() as ctx:
        keep = ctx.enter_context(tc.tile_pool(name="keep", bufs=1))
        raw = ctx.enter_context(tc.tile_pool(name="raw", bufs=4))
        turns = ctx.enter_context(tc.tile_pool(name="turns", bufs=1))
        psum = ctx.enter_context(tc.psum_pool(name="psum", bufs=8))

        picks = keep.tile([P, S // 16], U16, name="picks")
        nc.sync.dma_start(picks[:], offs)
        cells = keep.tile([P, S // 16], U16, name="cells")

        dummy = keep.tile([P, 1], F32, name="dummy")
        nc.gpsimd.memset(dummy[:], 0.0)
        dummy_out = keep.tile([P, 1], F32, name="dummy_out")
        nc.scalar.activation(dummy_out[:], dummy[:], RELU)

        z = []
        for i in range(8):
            zt = keep.tile([P, V], F32, name="z%d" % i)
            (nc.vector if i < 3 else nc.gpsimd).memset(zt[:], 0.0)
            z.append(zt)

        w1_codes = [keep.tile([P, HALF], U32, name="w1c%d" % g, align_bytes=64) for g in range(2)]
        w1_scales = [keep.tile([P, HALF], U8, name="w1s%d" % g, align_bytes=64) for g in range(2)]
        w2_codes = [keep.tile([P, N], U32, name="w2c%d" % g, align_bytes=64) for g in range(2)]
        w2_scales = [keep.tile([P, N], U8, name="w2s%d" % g, align_bytes=64) for g in range(2)]
        z_last = keep.tile([P, V, PACK], BF16, name="z_last", align_bytes=64)
        z_codes = [keep.tile([P, V], U32, name="zc%d" % g, align_bytes=64) for g in range(2)]
        z_scales = [keep.tile([P, V], U8, name="zs%d" % g, align_bytes=64) for g in range(2)]
        x_codes = keep.tile([P, S], U32, name="x_codes", align_bytes=64)
        x_scales = keep.tile([P, S], U8, name="x_scales", align_bytes=64)
        weights = keep.tile([P, S], F32, name="weights")

        def turn(tag, shape, dtype, name):
            return turns.tile(shape, dtype, name=name, tag=tag, align_bytes=64)

        w1_raw, w2_raw = [], []

        def regroup_w1(g, t0, t1, tag):
            wg = turn(tag, [P, t1 - t0, P, PACK], BF16, "w1g%d%d" % (g, t0))
            source = w1_raw[g][:].rearrange("p j (m t) -> p m t j", t=PACK)
            nc.scalar.copy(wg[:].rearrange("p t m j -> p m t j"), source[:, :, t0:t1, :])
            return wg

        def quantize_w1(g, t0, t1, wg):
            cols = slice(t0 * P, t1 * P)
            quantize(w1_codes[g][:, cols], w1_scales[g][:, cols], wg.rearrange("p t m j -> p (t m) j"))

        with tc.tile_pool(name="xpool", bufs=1) as xpool:
            x_rows = []
            for j in range(PACK):
                xr = xpool.tile([P, T], F32, name="x%d" % j)
                nc.sync.dma_start(xr[:], x_view[:, j, :])
                x_rows.append(xr)
            for g in range(2):
                wr = raw.tile([P, PACK, HALF], F32, name="raw")
                nc.sync.dma_start(wr[:], w1_view[:, :, g * HALF : (g + 1) * HALF])
                w1_raw.append(wr)
                if g == 0:
                    nc.sync.dma_start(weights[:], gate)
                    nc.sync.dma_start(cells[:], pos1)
            for g in range(2):
                wr = raw.tile([P, PACK, N], F32, name="raw")
                nc.sync.dma_start(wr[:], w2[g * HALF : (g + 1) * HALF, :].rearrange("(p j) n -> p j n", j=PACK))
                w2_raw.append(wr)

            gathered = xpool.tile([P, 2, S], F32, name="gathered")
            grouped = xpool.tile([P, S, PACK], BF16, name="grouped", align_bytes=64)
            for j in range(2):
                nc.vector.tensor_copy(gathered[:, j, :], x_rows[j][:].indirect(picks[:]))
            for a, b in PIECES:
                nc.scalar.copy(grouped[:, a:b, 0:2], gathered[:, :, a:b].rearrange("p j w -> p w j"))
            w1g0 = regroup_w1(0, 0, 1, "w1first")
            for j in (2, 3):
                for a, b in PIECES:
                    nc.vector.tensor_copy(grouped[:, a:b, j], x_rows[j][:].indirect(picks[:, a // 16 : b // 16]))
                    if j == 3:
                        quantize(x_codes[:, a:b], x_scales[:, a:b], grouped[:, a:b, :])
            quantize_w1(0, 0, 1, w1g0[:])

        fpool = ctx.enter_context(tc.tile_pool(name="fpool", bufs=1))
        front = [
            fpool.tile([P, 2, V], F32, name="front01"),
            fpool.tile([P, 2, V], F32, name="front23"),
        ]

        def first(i, a, b, tag, on_vector=False):
            g, t = divmod(i, PACK)
            cols = slice(t * P, (t + 1) * P)
            h = turn(tag, [P, b - a], F32, "h%d_%d" % (i, a))
            for a0, b0 in PIECES:
                if a <= a0 and b0 <= b:
                    bank = psum.tile([P, 512], F32, name="bank")
                    nc.tensor.matmul_mx(
                        out=bank[:, : b0 - a0],
                        lhsT=w1_codes[g][:, cols].bitcast(FP8X4),
                        lhsT_scale=w1_scales[g][:, cols],
                        rhs=x_codes[:, a0:b0].bitcast(FP8X4),
                        rhs_scale=x_scales[:, a0:b0],
                        start=True,
                        stop=True,
                    )
                    if on_vector:
                        nc.vector.tensor_scalar_max(h[:, a0 - a : b0 - a], bank[:, : b0 - a0], 0.0)
                    else:
                        nc.scalar.activation(h[:, a0 - a : b0 - a], bank[:, : b0 - a0], RELU)
            return h

        def scatter(i, a, b, h):
            nc.vector.tensor_tensor(z[i][:].indirect(cells[:, a // 16 : b // 16]), h[:], weights[:, a:b], MULT)

        def regroup_w2(g, tag):
            wg = turn(tag, [P, N, PACK], BF16, "w2g%d" % g)
            nc.scalar.copy(wg[:], w2_raw[g][:].rearrange("p j n -> p n j"))
            return wg

        def to_front(i):
            nc.sync.dma_start(front[i // 2][:, i % 2, :], z[i][:])

        def pair_up(i, target, t, lo, hi):
            for a in range(lo, hi, 512):
                nc.scalar.copy(
                    target[:, a - lo : a - lo + 512, t : t + 2],
                    front[i][:, :, a : a + 512].rearrange("p j w -> p w j"),
                )

        def second(bank, m, c, g):
            a, b = CHUNKS[c]
            cols = slice(m * P, (m + 1) * P)
            nc.tensor.matmul_mx(
                out=bank[:, : b - a],
                lhsT=w2_codes[g][:, cols].bitcast(FP8X4),
                lhsT_scale=w2_scales[g][:, cols],
                rhs=z_codes[g][:, a:b].bitcast(FP8X4),
                rhs_scale=z_scales[g][:, a:b],
                start=(g == 0),
                stop=(g == 1),
            )

        h0a = first(0, 0, 256, "h0a")
        w1g1 = regroup_w1(0, 1, 4, "w1g1")
        quantize_w1(0, 1, 2, w1g1[:, 0:1])
        quantize_w1(0, 2, 4, w1g1[:, 1:3])
        h0b = first(0, 256, S, "w1g1")
        scatter(0, 0, 256, h0a)
        h1 = first(1, 0, S, "h1")
        scatter(0, 256, S, h0b)
        to_front(0)
        w1gb = regroup_w1(1, 0, 4, "w1gb")
        quantize_w1(1, 0, 4, w1gb[:])
        h2 = first(2, 0, S, "w1gb")
        scatter(1, 0, S, h1)
        to_front(1)
        w2g0 = regroup_w2(0, "w2g0")
        quantize(w2_codes[0][:], w2_scales[0][:], w2g0[:])
        h3 = first(3, 0, S, "w2g0")
        scatter(2, 0, S, h2)
        to_front(2)
        w2g1 = regroup_w2(1, "w2g1")
        quantize(w2_codes[1][:], w2_scales[1][:], w2g1[:])
        h4 = first(4, 0, S, "w2g1")
        z_first = turn("z_first", [P, V, PACK], BF16, "z_first")
        pair_up(0, z_first, 0, 0, V)
        scatter(3, 0, S, h3)
        to_front(3)
        h5 = first(5, 0, S, "h5")
        h6 = first(6, 0, S, "h6")
        h7b = first(7, 256, S, "h7b")
        scatter(4, 0, S, h4)
        pair_up(1, z_first, 2, 0, V)
        nc.scalar.copy(z_last[:, 0:1, 0], front[1][:, 1, 0:1])
        nc.scalar.copy(z_last[:, :, 0], z[4][:])
        scatter(5, 0, S, h5)
        nc.scalar.copy(z_last[:, :, 1], z[5][:])
        for a, b in ((0, 1024), (1024, V)):
            quantize(z_codes[0][:, a:b], z_scales[0][:, a:b], z_first[:, a:b, :])
        h7a = first(7, 0, 256, "z_first", on_vector=True)
        banks = {}
        for c in (0, 2):
            for m in range(4):
                banks[c, m] = psum.tile([P, 512], F32, name="bank")
                second(banks[c, m], m, c, 0)
        scatter(6, 0, S, h6)
        for a, b in CHUNKS:
            nc.scalar.copy(z_last[:, a:b, 2], z[6][:, a:b])
            nc.scalar.copy(z_last[:, a : a + 1, 3], z[6][:, a : a + 1])
        scatter(7, 256, S, h7b)
        scatter(7, 0, 256, h7a)

        def last_plane(c):
            a, b = CHUNKS[c]
            nc.vector.tensor_copy(z_last[:, a:b, 3], z[7][:, a:b])

        def last_quantize(c):
            a, b = CHUNKS[c]
            quantize(z_codes[1][:, a:b], z_scales[1][:, a:b], z_last[:, a:b, :])

        def finish(c, copies):
            a, b = CHUNKS[c]
            staged = raw.tile([P, PACK, 512], F32, name="raw")
            for m in range(4):
                if (c, m) not in banks:
                    banks[c, m] = psum.tile([P, 512], F32, name="bank")
                    second(banks[c, m], m, c, 0)
                second(banks[c, m], m, c, 1)
                if copies[m] == "s":
                    nc.scalar.copy(staged[:, m, : b - a], banks[c, m][:, : b - a])
                else:
                    nc.vector.tensor_copy(staged[:, m, : b - a], banks[c, m][:, : b - a])
                if m % 2 == 1:
                    nc.sync.dma_start(out_view[:, m - 1 : m + 1, a:b], staged[:, m - 1 : m + 1, : b - a])

        last_plane(0)
        last_plane(1)
        last_quantize(0)
        last_plane(2)
        last_quantize(1)
        last_plane(3)
        last_quantize(2)
        last_quantize(3)
        finish(0, "ssss")
        finish(1, "ssss")
        finish(2, "ssvv")
        finish(3, "svsv")
